import numpy as np
import ml_dtypes


def mxq(x, axis, fmt="e4m3"):
    dtype, down = {"e4m3": (ml_dtypes.float8_e4m3fn, 7), "e5m2": (ml_dtypes.float8_e5m2, 14)}[fmt]
    v = np.moveaxis(np.asarray(x, np.float32).astype(ml_dtypes.bfloat16).astype(np.float64), axis, -1)
    blocks = v.reshape(v.shape[:-1] + (-1, 32))
    amax = np.abs(blocks).max(-1, keepdims=True)
    byte = np.maximum(np.where(amax > 0, np.frexp(amax)[1] - 1 + 127, 0) - down, 1)
    scale = np.exp2(byte - 127.0)
    codes = (blocks / scale).astype(np.float32).astype(dtype).astype(np.float64)
    return np.moveaxis((codes * scale).reshape(v.shape), -1, axis)


WIDE = False


def mx_kscale(k):
    if not WIDE:
        return np.ones(k)
    levels = np.array([10, -10, 5, -5, 0])
    if k % 512:
        return np.exp2(np.random.permutation(np.resize(levels, k // 32))).repeat(32)
    a = np.empty((k // 512, 16))
    for p in range(k // 512):
        a[p, :8] = np.random.permutation(np.resize(levels, 8))
        for g in range(8):
            far = levels[np.abs(levels - a[p, g]) >= 10]
            a[p, g + 8] = far[np.random.randint(len(far))]
    return np.exp2(a.ravel()).repeat(32)


def f64(x):
    return np.asarray(x).astype(np.float64)


def striped(idx):
    return np.tile(np.asarray(idx).reshape(-1, 16).T, (8, 1)).astype(np.uint16)


def unstriped(offs):
    return offs[:16].T.reshape(-1).astype(np.int64)


E2M1 = np.array([0.0, 0.5, 1.0, 1.5, 2.0, 3.0, 4.0, 6.0, -0.0, -0.5, -1.0, -1.5, -2.0, -3.0, -4.0, -6.0])


def pack_weight(w, fmt):
    k, n = w.shape
    w = f64(np.asarray(w, np.float32).astype(ml_dtypes.bfloat16)).reshape(k // 32, 32, n)
    amax = np.abs(w).max(1)
    if fmt == "e4m3":
        byte = np.frexp(amax)[1] - 1 + 127 - 7
    else:
        mant, ex = np.frexp(amax / 6.0)
        byte = np.where(mant > 0.5, ex, ex - 1) + 127
    byte = np.clip(np.where(amax > 0, byte, 1), 1, 254)
    scaled = (w * np.exp2(127.0 - byte)[:, None, :]).reshape(k, n).astype(np.float32)
    by_word = np.ascontiguousarray(scaled.reshape(k // 512, 128, 4, n).transpose(0, 1, 3, 2))
    if fmt == "e4m3":
        words = by_word.astype(ml_dtypes.float8_e4m3fn).view(np.uint8)
    else:
        c = by_word.astype(ml_dtypes.float4_e2m1fn).view(np.uint8) & 0xF
        words = (c[..., 0::2] | (c[..., 1::2] << 4)).reshape(k // 512, 128, 2 * n)
    return np.ascontiguousarray(words), np.ascontiguousarray(byte.astype(np.uint8).reshape(k // 512, 16, n))


def unpack_weight(words, scales, fmt):
    g, _, n = scales.shape
    words = np.ascontiguousarray(words).reshape(g, 128, n, -1)
    if fmt == "e4m3":
        vals = words.view(ml_dtypes.float8_e4m3fn).astype(np.float64)
    else:
        nib = np.empty((g, 128, n, 4), np.uint8)
        nib[..., 0::2] = words & 0xF
        nib[..., 1::2] = words >> 4
        vals = E2M1[nib]
    vals = vals * np.repeat(np.exp2(scales.astype(np.float64) - 127.0), 8, axis=1)[..., None]
    return vals.transpose(0, 1, 3, 2).reshape(g * 512, n)


B, N, T, D, DV, NQ = 2, 512, 2048, 1024, 256, 256


def setup_inputs():
    n = np.random.standard_normal
    seg = T // B
    idx = np.concatenate([b * seg + np.random.permutation(seg)[:N] for b in range(B)])
    s = mx_kscale(D)[:, None]
    u = np.ones(T)
    u[idx] = mx_kscale(B * N)
    r = np.random.uniform(0.5, 2.0, T)
    k = n((D, T)) / s
    v = n((DV, T)) / (u * r)
    kp = pack_weight(k, "e2m1")
    return {
        "qT": (n((B, D, NQ)) * s * (1.00 / np.sqrt(D))).astype(np.float32),
        "k_words": np.ascontiguousarray(kp[0].reshape(D // 1024, 2, 128, T, 2).transpose(0, 2, 3, 1, 4)).reshape(D // 1024, 128, T, 4),
        "k_scales": kp[1],
        "vT": v.astype(np.float32),
        "vs": np.tile(u * r, (128, 1)).astype(np.float32),
        "offs": striped(idx),
    }


def reference(qT, k_words, k_scales, vT, vs, offs):
    idx = unstriped(offs)
    k = unpack_weight(k_words.reshape(D // 1024, 128, T, 2, 2).transpose(0, 3, 1, 2, 4).reshape(D // 512, 128, 2 * T), k_scales, "e2m1")
    v = f64(vT)
    pick = lambda x: x[:, idx].reshape(x.shape[0], B, N).transpose(1, 0, 2)
    q = f64(qT)
    score = mxq(q, 1, "e4m3").transpose(0, 2, 1) @ pick(k)
    p = score / (1.0 + np.exp(-score))
    w = p * pick(f64(vs))[:, :1, :]
    y = mxq(w, 2, "e4m3") @ mxq(pick(v).transpose(0, 2, 1), 1, "e4m3")
    y = y / 16.0
    return y

@@ -1,0 +1,219 @@
+from contextlib import ExitStack
+
+import concourse.mybir as mybir
+from concourse.masks import make_identity
+
+B, N, T, D, DV, NQ = 2, 512, 2048, 1024, 256, 256
+FLOPS = 2 * B * NQ * N * (D + DV)
+BYTES = 4 * B * D * NQ + 4 * 128 * T + 32 * T + 4 * DV * T + 4 * T + 2 * 128 * 64 + 4 * B * NQ * DV
+
+F32 = mybir.dt.float32
+BF16 = mybir.dt.bfloat16
+I32 = mybir.dt.int32
+U32 = mybir.dt.uint32
+U16 = mybir.dt.uint16
+U8 = mybir.dt.uint8
+FP8X4 = mybir.dt.float8_e4m3fn_x4
+FP4X4 = mybir.dt.float4_e2m1fn_x4
+ACT = mybir.ActivationFunctionType
+MULT = mybir.AluOpType.mult
+
+P = 128
+SEG = T // B
+PASSES = D // 512
+COLS = N // 16
+
+
+def tile_attend_silu_seg_kernel(tc, qT, k_words, k_scales, vT, vs, offs, out):
+    nc = tc.nc
+    with ExitStack() as ctx:
+        held = ctx.enter_context(tc.tile_pool(name="held", bufs=1))
+        psum = ctx.enter_context(tc.psum_pool(name="psum", bufs=1))
+
+        def sb(shape, dtype, name):
+            return held.tile(shape, dtype, name=name, align_bytes=64)
+
+        offsets = held.tile([P, B * COLS], U16, name="offsets")
+        nc.sync.dma_start(offsets[:], offs)
+
+        scale_pool = sb([P, T], U8, "scale_pool")
+        scale_rows = k_scales.rearrange("o f t -> (o f) t").rearrange("(a h i) t -> h a i t", h=2, i=4)
+        for h in range(2):
+            nc.scalar.dma_start(scale_pool[32 * h + 16 : 32 * h + 32, :].bitcast(I32), scale_rows[h].bitcast(I32))
+        warm_in = sb([P, 1], F32, "warm_in")
+        nc.vector.memset(warm_in[:], 0.0)
+        for first, last in ((0, 16), (32, 48), (64, 128)):
+            nc.vector.memset(scale_pool[first:last, :].bitcast(I32), 0)
+        vs_pool = sb([P, T], F32, "vs_pool")
+        nc.vector.memset(vs_pool[0 : P - 1, :], 0.0)
+        warm = sb([P, 1], F32, "warm")
+        nc.scalar.activation(warm[:], warm_in[:], ACT.Silu)
+
+        word_pool = sb([P, T], I32, "word_pool")
+        words_hbm = k_words[0].rearrange("p t y -> p (t y)").bitcast(I32)
+        v_hbm = vT.rearrange("(h p) t -> p h t", h=2)
+        q_raw = [[sb([P, 4, NQ], F32, f"q_raw{b}{o}") for o in range(PASSES)] for b in range(B)]
+        v_raw = sb([P, 2, T], F32, "v_raw")
+        HALF = SEG // 2
+
+        def load_words(b):
+            nc.sync.dma_start(word_pool[:, b * SEG : (b + 1) * SEG], words_hbm[:, b * SEG : (b + 1) * SEG])
+
+        def load_q(b, o):
+            nc.sync.dma_start(q_raw[b][o][:], qT[b, 512 * o : 512 * (o + 1), :].rearrange("(p j) q -> p j q", j=4))
+
+        load_q(0, 0)
+        load_words(0)
+        nc.sync.dma_start(vs_pool[P - 1 : P, :], vs[0:1, :])
+        nc.sync.dma_start(v_raw[:, :, 0:HALF], v_hbm[:, :, 0:HALF])
+        load_q(0, 1)
+        nc.sync.dma_start(v_raw[:, :, HALF:SEG], v_hbm[:, :, HALF:SEG])
+        load_q(1, 0)
+        load_q(1, 1)
+        load_words(1)
+        for h in range(2):
+            nc.sync.dma_start(v_raw[:, h, SEG:T], v_hbm[:, h, SEG:T])
+
+        ident = sb([P, P], F32, "ident")
+        make_identity(nc, ident[:])
+        ident_bf = sb([P, P], BF16, "ident_bf")
+        make_identity(nc, ident_bf[:])
+
+        def listed(pool_ap, b):
+            return pool_ap[:, : (b + 1) * SEG].indirect(offsets[:, b * COLS : (b + 1) * COLS])
+
+        def dealt(ap):
+            return ap.rearrange("p (t g j) -> p g t j", t=4, g=16, j=8)
+
+        scale_got = sb([P, B * N], U8, "scale_got")
+        nc.vector.tensor_copy(scale_got[:], scale_pool[:].indirect(offsets[:]))
+        scale_dealt = sb([P, B * N], U8, "scale_dealt")
+        nc.vector.tensor_copy(
+            scale_dealt[:].bitcast(I32).rearrange("p (b t g w) -> p b t g w", b=B, t=4, g=16),
+            scale_got[:].bitcast(I32).rearrange("p (b g t w) -> p b t g w", b=B, t=4, g=16),
+        )
+
+        k_codes = []
+        for b in range(B):
+            words_got = sb([P, N], U32, f"words_got{b}")
+            nc.vector.tensor_copy(words_got[:], listed(word_pool[:].bitcast(U32), b))
+            codes = sb([P, PASSES * 2 * N], U8, f"k_codes{b}")
+            nc.vector.tensor_copy(
+                codes[:].bitcast(U16).rearrange("p (o t g j) -> p o t g j", o=2, t=4, g=16),
+                words_got[:].bitcast(U16).rearrange("p (g t j o) -> p o t g j", o=2, t=4, g=16),
+            )
+            k_codes.append(codes)
+
+        q_codes, q_plane = {}, {}
+
+        def quantise_q(b, o):
+            q_grouped = sb([P, NQ * 4], BF16, f"q_grouped{b}{o}")
+            nc.scalar.copy(
+                q_grouped[:].rearrange("p (c i t) -> p c t i", i=4, t=4),
+                q_raw[b][o][:].rearrange("p t (c i) -> p c t i", i=4),
+            )
+            q_codes[b, o] = sb([P, NQ], U32, f"q_codes{b}{o}")
+            q_plane[b, o] = sb([P, NQ], U8, f"q_plane{b}{o}")
+            nc.vector.quantize_mx(out=q_codes[b, o][:].bitcast(FP8X4), scales=q_plane[b, o][:], in_=q_grouped[:])
+
+        v_pairs = sb([P, 2 * SEG], BF16, "v_pairs")
+        quantise_q(0, 0)
+        for first in (0, HALF):
+            nc.scalar.copy(
+                v_pairs[:, 2 * first : 2 * (first + HALF)].rearrange("p (c i h) -> p c h i", i=4, h=2),
+                v_raw[:, :, first : first + HALF].rearrange("p h (c i) -> p c h i", i=4),
+            )
+        quantise_q(0, 1)
+        quantise_q(1, 0)
+        quantise_q(1, 1)
+
+        k_plane = [sb([P, B * N], U8, f"k_plane{o}") for o in range(PASSES)]
+        for o in range(PASSES):
+            for u in range(2):
+                first = 16 + 8 * o + 4 * u
+                nc.scalar.dma_start(
+                    k_plane[o][64 * u : 64 * u + 64, :].bitcast(I32),
+                    scale_dealt[first : first + 64, :].bitcast(I32),
+                )
+
+        silu = {}
+        for b in range(B):
+            for c in range(2):
+                bank = psum.tile([P, 4, P], F32, name=f"score_bank{b}{c}", tag=f"bank_s{b}{c}")
+                for t in range(4):
+                    for o in range(PASSES):
+                        nc.tensor.matmul_mx(
+                            out=bank[:, t, :],
+                            lhsT=k_codes[b][:, o * 2 * N + t * 2 * P : o * 2 * N + (t + 1) * 2 * P].bitcast(FP4X4),
+                            lhsT_scale=k_plane[o][:, b * N + t * P : b * N + (t + 1) * P],
+                            rhs=q_codes[b, o][:, c * P : (c + 1) * P].bitcast(FP8X4),
+                            rhs_scale=q_plane[b, o][:, c * P : (c + 1) * P],
+                            start=(o == 0),
+                            stop=(o == PASSES - 1),
+                        )
+                silu[b, c] = sb([P, P, 4], F32, f"p{b}{c}")
+                nc.scalar.activation(silu[b, c][:], bank[:].rearrange("p t q -> p q t"), ACT.Silu)
+
+        vs_col = []
+        for b in range(B):
+            vs_got = sb([P, N], F32, f"vs_got{b}")
+            nc.vector.tensor_copy(dealt(vs_got[:].bitcast(U32)), listed(vs_pool[:].bitcast(U32), b))
+            bank = psum.tile([P, 4, P], F32, name=f"vs_bank{b}", tag=f"bank_a{b}")
+            for t in range(4):
+                nc.tensor.transpose(bank[:, t, :], vs_got[:, t * P : (t + 1) * P], ident[:])
+            col = sb([P, 4], F32, f"vs_col{b}")
+            nc.scalar.copy(col[:], bank[:, :, P - 1])
+            vs_col.append(col)
+
+        v_grouped = [sb([P, DV * 4], BF16, f"v_grouped{b}") for b in range(B)]
+        v_codes = [sb([P, DV], U32, f"v_codes{b}") for b in range(B)]
+        v_plane = [sb([P, DV], U8, f"v_plane{b}") for b in range(B)]
+
+        for h in range(2):
+            v_got = sb([P, N], BF16, f"v_got1{h}")
+            nc.vector.tensor_copy(dealt(v_got[:]), listed(v_raw[:, h, :], 1))
+            bank = psum.tile([P, 4, P], BF16, name=f"v_bank1{h}", tag=f"bank_a{h}")
+            for t in range(4):
+                nc.tensor.transpose(bank[:, t, :], v_got[:, t * P : (t + 1) * P], ident_bf[:])
+            nc.scalar.copy(
+                v_grouped[1][:, h * 4 * P : (h + 1) * 4 * P].rearrange("p (m t) -> p m t", t=4),
+                bank[:].rearrange("p t m -> p m t"),
+            )
+        nc.vector.quantize_mx(out=v_codes[1][:].bitcast(FP8X4), scales=v_plane[1][:], in_=v_grouped[1][:])
+
+        v_got = sb([P, N], F32, "v_got0")
+        nc.vector.tensor_copy(dealt(v_got[:].bitcast(U32)), listed(v_pairs[:].bitcast(U32), 0))
+        bank = psum.tile([P, 4, P], F32, name="v_bank0", tag="bank_v")
+        for t in range(4):
+            nc.tensor.transpose(bank[:, t, :], v_got[:, t * P : (t + 1) * P], ident[:])
+        nc.scalar.copy(
+            v_grouped[0][:].rearrange("p (h m t) -> p h m t", h=2, t=4),
+            bank[:].rearrange("p t m -> p (t m)").bitcast(BF16).rearrange("p (t m h) -> p h m t", t=4, h=2),
+        )
+        nc.vector.quantize_mx(out=v_codes[0][:].bitcast(FP8X4), scales=v_plane[0][:], in_=v_grouped[0][:])
+
+        for b in range(B):
+            w_grouped = []
+            for c in range(2):
+                w = sb([P, P, 4], BF16, f"w{b}{c}")
+                nc.vector.tensor_tensor(w[:], silu[b, c][:], vs_col[b][:].unsqueeze(1).to_broadcast([P, P, 4]), MULT)
+                w_grouped.append(w)
+            for c in range(2):
+                w_codes = sb([P, P], U32, f"w_codes{b}{c}")
+                w_plane = sb([P, P], U8, f"w_plane{b}{c}")
+                nc.vector.quantize_mx(
+                    out=w_codes[:].bitcast(FP8X4), scales=w_plane[:], in_=w_grouped[c][:].rearrange("p q t -> p (q t)")
+                )
+                bank = psum.tile([P, DV], F32, name=f"y_bank{b}{c}", tag=f"bank_s{b}{c}")
+                nc.tensor.matmul_mx(
+                    out=bank[:],
+                    lhsT=w_codes[:].bitcast(FP8X4),
+                    lhsT_scale=w_plane[:],
+                    rhs=v_codes[b][:].bitcast(FP8X4),
+                    rhs_scale=v_plane[b][:],
+                    start=True,
+                    stop=True,
+                )
+                y = sb([P, DV], F32, f"y{b}{c}")
+                nc.scalar.activation(y[:], bank[:], ACT.Copy, scale=1.0 / 16.0)
+                nc.sync.dma_start(out[b, c * P : (c + 1) * P, :], y[:])

@@ -31,21 +31,21 @@ def tile_attend_silu_seg_kernel(tc, qT, k_words, k_scales, vT, vs, offs, out):
         psum = ctx.enter_context(tc.psum_pool(name="psum", bufs=1))
 
         def sb(shape, dtype, name):
-            return held.tile(shape, dtype, name=name, align_bytes=64)
+            return held.tile(shape, dtype, name=name, tag=name, align_bytes=64)
 
         offsets = held.tile([P, B * COLS], U16, name="offsets")
         nc.sync.dma_start(offsets[:], offs)
 
-        scale_pool = sb([P, T], U8, "scale_pool")
+        scale_pool = sb([P, T + 4], U8, "scale_pool")
         scale_rows = k_scales.rearrange("o f t -> (o f) t").rearrange("(a h i) t -> h a i t", h=2, i=4)
         for h in range(2):
-            nc.scalar.dma_start(scale_pool[32 * h + 16 : 32 * h + 32, :].bitcast(I32), scale_rows[h].bitcast(I32))
+            nc.sync.dma_start(scale_pool[32 * h + 16 : 32 * h + 32, 0:T].bitcast(I32), scale_rows[h].bitcast(I32))
+        vs_pool = sb([P, T], F32, "vs_pool")
+        nc.gpsimd.memset(vs_pool[0 : P - 1, :], 0.0)
         warm_in = sb([P, 1], F32, "warm_in")
         nc.vector.memset(warm_in[:], 0.0)
         for first, last in ((0, 16), (32, 48), (64, 128)):
             nc.vector.memset(scale_pool[first:last, :].bitcast(I32), 0)
-        vs_pool = sb([P, T], F32, "vs_pool")
-        nc.vector.memset(vs_pool[0 : P - 1, :], 0.0)
         warm = sb([P, 1], F32, "warm")
         nc.scalar.activation(warm[:], warm_in[:], ACT.Silu)
 
@@ -53,7 +53,7 @@ def tile_attend_silu_seg_kernel(tc, qT, k_words, k_scales, vT, vs, offs, out):
         words_hbm = k_words[0].rearrange("p t y -> p (t y)").bitcast(I32)
         v_hbm = vT.rearrange("(h p) t -> p h t", h=2)
         q_raw = [[sb([P, 4, NQ], F32, f"q_raw{b}{o}") for o in range(PASSES)] for b in range(B)]
-        v_raw = sb([P, 2, T], F32, "v_raw")
+        v_raw = sb([P, 2 * T], F32, "v_raw")
         HALF = SEG // 2
 
         def load_words(b):
@@ -65,19 +65,15 @@ def tile_attend_silu_seg_kernel(tc, qT, k_words, k_scales, vT, vs, offs, out):
         load_q(0, 0)
         load_words(0)
         nc.sync.dma_start(vs_pool[P - 1 : P, :], vs[0:1, :])
-        nc.sync.dma_start(v_raw[:, :, 0:HALF], v_hbm[:, :, 0:HALF])
+        nc.sync.dma_start(v_raw[:, 0:SEG].rearrange("p (h t) -> p h t", h=2), v_hbm[:, :, 0:HALF])
         load_q(0, 1)
-        nc.sync.dma_start(v_raw[:, :, HALF:SEG], v_hbm[:, :, HALF:SEG])
+        nc.sync.dma_start(v_raw[:, SEG:T].rearrange("p (h t) -> p h t", h=2), v_hbm[:, :, HALF:SEG])
         load_q(1, 0)
-        load_q(1, 1)
-        load_words(1)
-        for h in range(2):
-            nc.sync.dma_start(v_raw[:, h, SEG:T], v_hbm[:, h, SEG:T])
 
         ident = sb([P, P], F32, "ident")
         make_identity(nc, ident[:])
         ident_bf = sb([P, P], BF16, "ident_bf")
-        make_identity(nc, ident_bf[:])
+        nc.scalar.copy(ident_bf[:], ident[:])
 
         def listed(pool_ap, b):
             return pool_ap[:, : (b + 1) * SEG].indirect(offsets[:, b * COLS : (b + 1) * COLS])
@@ -86,12 +82,26 @@ def tile_attend_silu_seg_kernel(tc, qT, k_words, k_scales, vT, vs, offs, out):
             return ap.rearrange("p (t g j) -> p g t j", t=4, g=16, j=8)
 
         scale_got = sb([P, B * N], U8, "scale_got")
-        nc.vector.tensor_copy(scale_got[:], scale_pool[:].indirect(offsets[:]))
+        nc.vector.tensor_copy(scale_got[:], scale_pool[:, 0:T].indirect(offsets[:]))
         scale_dealt = sb([P, B * N], U8, "scale_dealt")
         nc.vector.tensor_copy(
             scale_dealt[:].bitcast(I32).rearrange("p (b t g w) -> p b t g w", b=B, t=4, g=16),
             scale_got[:].bitcast(I32).rearrange("p (b g t w) -> p b t g w", b=B, t=4, g=16),
         )
+
+        k_plane = [sb([P, B * N], U8, f"k_plane{o}") for o in range(PASSES)]
+        for o in range(PASSES):
+            for u in range(2):
+                first = 16 + 8 * o + 4 * u
+                nc.sync.dma_start(
+                    k_plane[o][64 * u : 64 * u + 64, :].bitcast(I32),
+                    scale_dealt[first : first + 64, :].bitcast(I32),
+                )
+
+        load_q(1, 1)
+        load_words(1)
+        for h in range(2):
+            nc.sync.dma_start(v_raw[:, T + h * SEG : T + (h + 1) * SEG], v_hbm[:, h, SEG:T])
 
         k_codes = []
         for b in range(B):
@@ -121,23 +131,15 @@ def tile_attend_silu_seg_kernel(tc, qT, k_words, k_scales, vT, vs, offs, out):
         for first in (0, HALF):
             nc.scalar.copy(
                 v_pairs[:, 2 * first : 2 * (first + HALF)].rearrange("p (c i h) -> p c h i", i=4, h=2),
-                v_raw[:, :, first : first + HALF].rearrange("p h (c i) -> p c h i", i=4),
+                v_raw[:, 2 * first : 2 * (first + HALF)].rearrange("p (h c i) -> p c h i", h=2, i=4),
             )
         quantise_q(0, 1)
         quantise_q(1, 0)
         quantise_q(1, 1)
 
-        k_plane = [sb([P, B * N], U8, f"k_plane{o}") for o in range(PASSES)]
-        for o in range(PASSES):
-            for u in range(2):
-                first = 16 + 8 * o + 4 * u
-                nc.scalar.dma_start(
-                    k_plane[o][64 * u : 64 * u + 64, :].bitcast(I32),
-                    scale_dealt[first : first + 64, :].bitcast(I32),
-                )
-
         silu = {}
         for b in range(B):
+            p_tile = held.tile([P, 2, P, 4], F32, name=f"p{b}", tag=f"q_raw1{1 - b}", align_bytes=64)
             for c in range(2):
                 bank = psum.tile([P, 4, P], F32, name=f"score_bank{b}{c}", tag=f"bank_s{b}{c}")
                 for t in range(4):
@@ -151,27 +153,29 @@ def tile_attend_silu_seg_kernel(tc, qT, k_words, k_scales, vT, vs, offs, out):
                             start=(o == 0),
                             stop=(o == PASSES - 1),
                         )
-                silu[b, c] = sb([P, P, 4], F32, f"p{b}{c}")
-                nc.scalar.activation(silu[b, c][:], bank[:].rearrange("p t q -> p q t"), ACT.Silu)
+                silu[b, c] = p_tile[:, c, :, :]
+                nc.scalar.activation(silu[b, c], bank[:].rearrange("p t q -> p q t"), ACT.Silu)
 
         vs_col = []
+        vs_bank = psum.tile([P, P + 4 * B], F32, name="vs_bank", tag="bank_vs")
         for b in range(B):
             vs_got = sb([P, N], F32, f"vs_got{b}")
             nc.vector.tensor_copy(dealt(vs_got[:].bitcast(U32)), listed(vs_pool[:].bitcast(U32), b))
-            bank = psum.tile([P, 4, P], F32, name=f"vs_bank{b}", tag=f"bank_a{b}")
-            for t in range(4):
-                nc.tensor.transpose(bank[:, t, :], vs_got[:, t * P : (t + 1) * P], ident[:])
-            col = sb([P, 4], F32, f"vs_col{b}")
-            nc.scalar.copy(col[:], bank[:, :, P - 1])
-            vs_col.append(col)
+            first = 4 * (B - 1 - b) + 1
+            for t in reversed(range(4)):
+                nc.tensor.transpose(vs_bank[:, first + t : first + t + P], vs_got[:, t * P : (t + 1) * P], ident[:])
+            vs_col.append(vs_bank[:, first + P - 1 : first + P + 3])
 
-        v_grouped = [sb([P, DV * 4], BF16, f"v_grouped{b}") for b in range(B)]
+        v_grouped = [
+            held.tile([P, DV * 4], BF16, name="v_grouped0", tag="q_grouped11", align_bytes=64),
+            sb([P, DV * 4], BF16, "v_grouped1"),
+        ]
         v_codes = [sb([P, DV], U32, f"v_codes{b}") for b in range(B)]
         v_plane = [sb([P, DV], U8, f"v_plane{b}") for b in range(B)]
 
         for h in range(2):
             v_got = sb([P, N], BF16, f"v_got1{h}")
-            nc.vector.tensor_copy(dealt(v_got[:]), listed(v_raw[:, h, :], 1))
+            nc.vector.tensor_copy(dealt(v_got[:]), listed(v_raw[:, (h + 1) * SEG : (h + 3) * SEG], 1))
             bank = psum.tile([P, 4, P], BF16, name=f"v_bank1{h}", tag=f"bank_a{h}")
             for t in range(4):
                 nc.tensor.transpose(bank[:, t, :], v_got[:, t * P : (t + 1) * P], ident_bf[:])
@@ -196,7 +200,7 @@ def tile_attend_silu_seg_kernel(tc, qT, k_words, k_scales, vT, vs, offs, out):
             w_grouped = []
             for c in range(2):
                 w = sb([P, P, 4], BF16, f"w{b}{c}")
-                nc.vector.tensor_tensor(w[:], silu[b, c][:], vs_col[b][:].unsqueeze(1).to_broadcast([P, P, 4]), MULT)
+                nc.vector.tensor_tensor(w[:], silu[b, c], vs_col[b].unsqueeze(1).to_broadcast([P, P, 4]), MULT)
                 w_grouped.append(w)
             for c in range(2):
                 w_codes = sb([P, P], U32, f"w_codes{b}{c}")

@@ -36,12 +36,16 @@ def tile_attend_silu_seg_kernel(tc, qT, k_words, k_scales, vT, vs, offs, out):
         offsets = held.tile([P, B * COLS], U16, name="offsets")
         nc.sync.dma_start(offsets[:], offs)
 
+        vs_pool = sb([P, T], F32, "vs_pool")
+        nc.sync.dma_start(vs_pool[P - 1 : P, :], vs[0:1, :])
         scale_pool = sb([P, T + 4], U8, "scale_pool")
         scale_rows = k_scales.rearrange("o f t -> (o f) t").rearrange("(a h i) t -> h a i t", h=2, i=4)
         for h in range(2):
             nc.sync.dma_start(scale_pool[32 * h + 16 : 32 * h + 32, 0:T].bitcast(I32), scale_rows[h].bitcast(I32))
-        vs_pool = sb([P, T], F32, "vs_pool")
-        nc.gpsimd.memset(vs_pool[0 : P - 1, :], 0.0)
+        ident = sb([P, P], F32, "ident")
+        nc.gpsimd.memset(vs_pool[0 : P - 1, 0:SEG], 0.0)
+        make_identity(nc, ident[:])
+        nc.gpsimd.memset(vs_pool[0 : P - 1, SEG:T], 0.0)
         warm_in = sb([P, 1], F32, "warm_in")
         nc.vector.memset(warm_in[:], 0.0)
         for first, last in ((0, 16), (32, 48), (64, 128)):
@@ -62,16 +66,14 @@ def tile_attend_silu_seg_kernel(tc, qT, k_words, k_scales, vT, vs, offs, out):
         def load_q(b, o):
             nc.sync.dma_start(q_raw[b][o][:], qT[b, 512 * o : 512 * (o + 1), :].rearrange("(p j) q -> p j q", j=4))
 
+        nc.sync.dma_start(v_raw[:, 0:SEG].rearrange("p (h t) -> p h t", h=2), v_hbm[:, :, 0:HALF])
+        nc.sync.dma_start(v_raw[:, SEG:T].rearrange("p (h t) -> p h t", h=2), v_hbm[:, :, HALF:SEG])
         load_q(0, 0)
         load_words(0)
-        nc.sync.dma_start(vs_pool[P - 1 : P, :], vs[0:1, :])
-        nc.sync.dma_start(v_raw[:, 0:SEG].rearrange("p (h t) -> p h t", h=2), v_hbm[:, :, 0:HALF])
         load_q(0, 1)
-        nc.sync.dma_start(v_raw[:, SEG:T].rearrange("p (h t) -> p h t", h=2), v_hbm[:, :, HALF:SEG])
         load_q(1, 0)
+        load_words(1)
 
-        ident = sb([P, P], F32, "ident")
-        make_identity(nc, ident[:])
         ident_bf = sb([P, P], BF16, "ident_bf")
         nc.scalar.copy(ident_bf[:], ident[:])
 
@@ -99,7 +101,6 @@ def tile_attend_silu_seg_kernel(tc, qT, k_words, k_scales, vT, vs, offs, out):
                 )
 
         load_q(1, 1)
-        load_words(1)
         for h in range(2):
             nc.sync.dma_start(v_raw[:, T + h * SEG : T + (h + 1) * SEG], v_hbm[:, h, SEG:T])
 
@@ -139,7 +140,7 @@ def tile_attend_silu_seg_kernel(tc, qT, k_words, k_scales, vT, vs, offs, out):
 
         silu = {}
         for b in range(B):
-            p_tile = held.tile([P, 2, P, 4], F32, name=f"p{b}", tag=f"q_raw1{1 - b}", align_bytes=64)
+            p_tile = held.tile([P, 2, P, 4], F32, name=f"p{b}", tag="q_raw11" if b == 0 else "p1", align_bytes=64)
             for c in range(2):
                 bank = psum.tile([P, 4, P], F32, name=f"score_bank{b}{c}", tag=f"bank_s{b}{c}")
                 for t in range(4):
@@ -167,7 +168,7 @@ def tile_attend_silu_seg_kernel(tc, qT, k_words, k_scales, vT, vs, offs, out):
             vs_col.append(vs_bank[:, first + P - 1 : first + P + 3])
 
         v_grouped = [
-            held.tile([P, DV * 4], BF16, name="v_grouped0", tag="q_grouped11", align_bytes=64),
+            held.tile([P, DV * 4], BF16, name="v_grouped0", tag="q_raw10", align_bytes=64),
             sb([P, DV * 4], BF16, "v_grouped1"),
         ]
         v_codes = [sb([P, DV], U32, f"v_codes{b}") for b in range(B)]
@@ -197,16 +198,14 @@ def tile_attend_silu_seg_kernel(tc, qT, k_words, k_scales, vT, vs, offs, out):
         nc.vector.quantize_mx(out=v_codes[0][:].bitcast(FP8X4), scales=v_plane[0][:], in_=v_grouped[0][:])
 
         for b in range(B):
-            w_grouped = []
+            w = held.tile([P, 2, P, 4], BF16, name=f"w{b}", tag="v_raw" if b == 0 else "w1", align_bytes=64)
             for c in range(2):
-                w = sb([P, P, 4], BF16, f"w{b}{c}")
-                nc.vector.tensor_tensor(w[:], silu[b, c], vs_col[b].unsqueeze(1).to_broadcast([P, P, 4]), MULT)
-                w_grouped.append(w)
+                nc.vector.tensor_tensor(w[:, c, :, :], silu[b, c], vs_col[b].unsqueeze(1).to_broadcast([P, P, 4]), MULT)
             for c in range(2):
                 w_codes = sb([P, P], U32, f"w_codes{b}{c}")
                 w_plane = sb([P, P], U8, f"w_plane{b}{c}")
                 nc.vector.quantize_mx(
-                    out=w_codes[:].bitcast(FP8X4), scales=w_plane[:], in_=w_grouped[c][:].rearrange("p q t -> p (q t)")
+                    out=w_codes[:].bitcast(FP8X4), scales=w_plane[:], in_=w[:, c, :, :].rearrange("p q t -> p (q t)")
                 )
                 bank = psum.tile([P, DV], F32, name=f"y_bank{b}{c}", tag=f"bank_s{b}{c}")
                 nc.tensor.matmul_mx(

from contextlib import ExitStack

import concourse.mybir as mybir
from concourse.masks import make_identity

B, N, T, D, DV, NQ = 2, 512, 2048, 1024, 256, 256
FLOPS = 2 * B * NQ * N * (D + DV)
BYTES = 4 * B * D * NQ + 4 * 128 * T + 32 * T + 4 * DV * T + 4 * T + 2 * 128 * 64 + 4 * B * NQ * DV

F32 = mybir.dt.float32
BF16 = mybir.dt.bfloat16
I32 = mybir.dt.int32
U32 = mybir.dt.uint32
U16 = mybir.dt.uint16
U8 = mybir.dt.uint8
FP8X4 = mybir.dt.float8_e4m3fn_x4
FP4X4 = mybir.dt.float4_e2m1fn_x4
ACT = mybir.ActivationFunctionType
MULT = mybir.AluOpType.mult

P = 128
SEG = T // B
PASSES = D // 512
COLS = N // 16


def tile_attend_silu_seg_kernel(tc, qT, k_words, k_scales, vT, vs, offs, out):
    nc = tc.nc
    with ExitStack() as ctx:
        held = ctx.enter_context(tc.tile_pool(name="held", bufs=1))
        psum = ctx.enter_context(tc.psum_pool(name="psum", bufs=1))

        def sb(shape, dtype, name):
            return held.tile(shape, dtype, name=name, tag=name, align_bytes=64)

        offsets = held.tile([P, B * COLS], U16, name="offsets")
        nc.sync.dma_start(offsets[:], offs)

        vs_pool = sb([P, T], F32, "vs_pool")
        nc.sync.dma_start(vs_pool[P - 1 : P, :], vs[0:1, :])
        scale_pool = sb([P, T + 4], U8, "scale_pool")
        scale_rows = k_scales.rearrange("o f t -> (o f) t").rearrange("(a h i) t -> h a i t", h=2, i=4)
        for h in range(2):
            nc.sync.dma_start(scale_pool[32 * h + 16 : 32 * h + 32, 0:T].bitcast(I32), scale_rows[h].bitcast(I32))
        ident = sb([P, P], F32, "ident")
        nc.gpsimd.memset(vs_pool[0 : P - 1, 0:SEG], 0.0)
        make_identity(nc, ident[:])
        nc.gpsimd.memset(vs_pool[0 : P - 1, SEG:T], 0.0)
        warm_in = sb([P, 1], F32, "warm_in")
        nc.vector.memset(warm_in[:], 0.0)
        for first, last in ((0, 16), (32, 48), (64, 128)):
            nc.vector.memset(scale_pool[first:last, :].bitcast(I32), 0)
        warm = sb([P, 1], F32, "warm")
        nc.scalar.activation(warm[:], warm_in[:], ACT.Silu)

        word_pool = sb([P, T], I32, "word_pool")
        words_hbm = k_words[0].rearrange("p t y -> p (t y)").bitcast(I32)
        v_hbm = vT.rearrange("(h p) t -> p h t", h=2)
        q_raw = [[sb([P, 4, NQ], F32, f"q_raw{b}{o}") for o in range(PASSES)] for b in range(B)]
        v_raw = sb([P, 2 * T], F32, "v_raw")
        HALF = SEG // 2

        def load_words(b):
            nc.sync.dma_start(word_pool[:, b * SEG : (b + 1) * SEG], words_hbm[:, b * SEG : (b + 1) * SEG])

        def load_q(b, o):
            nc.sync.dma_start(q_raw[b][o][:], qT[b, 512 * o : 512 * (o + 1), :].rearrange("(p j) q -> p j q", j=4))

        nc.sync.dma_start(v_raw[:, 0:SEG].rearrange("p (h t) -> p h t", h=2), v_hbm[:, :, 0:HALF])
        nc.sync.dma_start(v_raw[:, SEG:T].rearrange("p (h t) -> p h t", h=2), v_hbm[:, :, HALF:SEG])
        load_q(0, 0)
        load_words(0)
        load_q(0, 1)
        load_q(1, 0)
        load_words(1)

        ident_bf = sb([P, P], BF16, "ident_bf")
        nc.scalar.copy(ident_bf[:], ident[:])

        def listed(pool_ap, b):
            return pool_ap[:, : (b + 1) * SEG].indirect(offsets[:, b * COLS : (b + 1) * COLS])

        def dealt(ap):
            return ap.rearrange("p (t g j) -> p g t j", t=4, g=16, j=8)

        scale_got = sb([P, B * N], U8, "scale_got")
        nc.vector.tensor_copy(scale_got[:], scale_pool[:, 0:T].indirect(offsets[:]))
        scale_dealt = sb([P, B * N], U8, "scale_dealt")
        nc.vector.tensor_copy(
            scale_dealt[:].bitcast(I32).rearrange("p (b t g w) -> p b t g w", b=B, t=4, g=16),
            scale_got[:].bitcast(I32).rearrange("p (b g t w) -> p b t g w", b=B, t=4, g=16),
        )

        k_plane = [sb([P, B * N], U8, f"k_plane{o}") for o in range(PASSES)]
        for o in range(PASSES):
            for u in range(2):
                first = 16 + 8 * o + 4 * u
                nc.sync.dma_start(
                    k_plane[o][64 * u : 64 * u + 64, :].bitcast(I32),
                    scale_dealt[first : first + 64, :].bitcast(I32),
                )

        load_q(1, 1)
        for h in range(2):
            nc.sync.dma_start(v_raw[:, T + h * SEG : T + (h + 1) * SEG], v_hbm[:, h, SEG:T])

        k_codes = []
        for b in range(B):
            words_got = sb([P, N], U32, f"words_got{b}")
            nc.vector.tensor_copy(words_got[:], listed(word_pool[:].bitcast(U32), b))
            codes = sb([P, PASSES * 2 * N], U8, f"k_codes{b}")
            nc.vector.tensor_copy(
                codes[:].bitcast(U16).rearrange("p (o t g j) -> p o t g j", o=2, t=4, g=16),
                words_got[:].bitcast(U16).rearrange("p (g t j o) -> p o t g j", o=2, t=4, g=16),
            )
            k_codes.append(codes)

        q_codes, q_plane = {}, {}

        def quantise_q(b, o):
            q_grouped = sb([P, NQ * 4], BF16, f"q_grouped{b}{o}")
            nc.scalar.copy(
                q_grouped[:].rearrange("p (c i t) -> p c t i", i=4, t=4),
                q_raw[b][o][:].rearrange("p t (c i) -> p c t i", i=4),
            )
            q_codes[b, o] = sb([P, NQ], U32, f"q_codes{b}{o}")
            q_plane[b, o] = sb([P, NQ], U8, f"q_plane{b}{o}")
            nc.vector.quantize_mx(out=q_codes[b, o][:].bitcast(FP8X4), scales=q_plane[b, o][:], in_=q_grouped[:])

        v_pairs = sb([P, 2 * SEG], BF16, "v_pairs")
        quantise_q(0, 0)
        for first in (0, HALF):
            nc.scalar.copy(
                v_pairs[:, 2 * first : 2 * (first + HALF)].rearrange("p (c i h) -> p c h i", i=4, h=2),
                v_raw[:, 2 * first : 2 * (first + HALF)].rearrange("p (h c i) -> p c h i", h=2, i=4),
            )
        quantise_q(0, 1)
        quantise_q(1, 0)
        quantise_q(1, 1)

        silu = {}
        for b in range(B):
            p_tile = held.tile([P, 2, P, 4], F32, name=f"p{b}", tag="q_raw11" if b == 0 else "p1", align_bytes=64)
            for c in range(2):
                bank = psum.tile([P, 4, P], F32, name=f"score_bank{b}{c}", tag=f"bank_s{b}{c}")
                for t in range(4):
                    for o in range(PASSES):
                        nc.tensor.matmul_mx(
                            out=bank[:, t, :],
                            lhsT=k_codes[b][:, o * 2 * N + t * 2 * P : o * 2 * N + (t + 1) * 2 * P].bitcast(FP4X4),
                            lhsT_scale=k_plane[o][:, b * N + t * P : b * N + (t + 1) * P],
                            rhs=q_codes[b, o][:, c * P : (c + 1) * P].bitcast(FP8X4),
                            rhs_scale=q_plane[b, o][:, c * P : (c + 1) * P],
                            start=(o == 0),
                            stop=(o == PASSES - 1),
                        )
                silu[b, c] = p_tile[:, c, :, :]
                nc.scalar.activation(silu[b, c], bank[:].rearrange("p t q -> p q t"), ACT.Silu)

        vs_col = []
        vs_bank = psum.tile([P, P + 4 * B], F32, name="vs_bank", tag="bank_vs")
        for b in range(B):
            vs_got = sb([P, N], F32, f"vs_got{b}")
            nc.vector.tensor_copy(dealt(vs_got[:].bitcast(U32)), listed(vs_pool[:].bitcast(U32), b))
            first = 4 * (B - 1 - b) + 1
            for t in reversed(range(4)):
                nc.tensor.transpose(vs_bank[:, first + t : first + t + P], vs_got[:, t * P : (t + 1) * P], ident[:])
            vs_col.append(vs_bank[:, first + P - 1 : first + P + 3])

        v_grouped = [
            held.tile([P, DV * 4], BF16, name="v_grouped0", tag="q_raw10", align_bytes=64),
            sb([P, DV * 4], BF16, "v_grouped1"),
        ]
        v_codes = [sb([P, DV], U32, f"v_codes{b}") for b in range(B)]
        v_plane = [sb([P, DV], U8, f"v_plane{b}") for b in range(B)]

        for h in range(2):
            v_got = sb([P, N], BF16, f"v_got1{h}")
            nc.vector.tensor_copy(dealt(v_got[:]), listed(v_raw[:, (h + 1) * SEG : (h + 3) * SEG], 1))
            bank = psum.tile([P, 4, P], BF16, name=f"v_bank1{h}", tag=f"bank_a{h}")
            for t in range(4):
                nc.tensor.transpose(bank[:, t, :], v_got[:, t * P : (t + 1) * P], ident_bf[:])
            nc.scalar.copy(
                v_grouped[1][:, h * 4 * P : (h + 1) * 4 * P].rearrange("p (m t) -> p m t", t=4),
                bank[:].rearrange("p t m -> p m t"),
            )
        nc.vector.quantize_mx(out=v_codes[1][:].bitcast(FP8X4), scales=v_plane[1][:], in_=v_grouped[1][:])

        v_got = sb([P, N], F32, "v_got0")
        nc.vector.tensor_copy(dealt(v_got[:].bitcast(U32)), listed(v_pairs[:].bitcast(U32), 0))
        bank = psum.tile([P, 4, P], F32, name="v_bank0", tag="bank_v")
        for t in range(4):
            nc.tensor.transpose(bank[:, t, :], v_got[:, t * P : (t + 1) * P], ident[:])
        nc.scalar.copy(
            v_grouped[0][:].rearrange("p (h m t) -> p h m t", h=2, t=4),
            bank[:].rearrange("p t m -> p (t m)").bitcast(BF16).rearrange("p (t m h) -> p h m t", t=4, h=2),
        )
        nc.vector.quantize_mx(out=v_codes[0][:].bitcast(FP8X4), scales=v_plane[0][:], in_=v_grouped[0][:])

        for b in range(B):
            w = held.tile([P, 2, P, 4], BF16, name=f"w{b}", tag="v_raw" if b == 0 else "w1", align_bytes=64)
            for c in range(2):
                nc.vector.tensor_tensor(w[:, c, :, :], silu[b, c], vs_col[b].unsqueeze(1).to_broadcast([P, P, 4]), MULT)
            for c in range(2):
                w_codes = sb([P, P], U32, f"w_codes{b}{c}")
                w_plane = sb([P, P], U8, f"w_plane{b}{c}")
                nc.vector.quantize_mx(
                    out=w_codes[:].bitcast(FP8X4), scales=w_plane[:], in_=w[:, c, :, :].rearrange("p q t -> p (q t)")
                )
                bank = psum.tile([P, DV], F32, name=f"y_bank{b}{c}", tag=f"bank_s{b}{c}")
                nc.tensor.matmul_mx(
                    out=bank[:],
                    lhsT=w_codes[:].bitcast(FP8X4),
                    lhsT_scale=w_plane[:],
                    rhs=v_codes[b][:].bitcast(FP8X4),
                    rhs_scale=v_plane[b][:],
                    start=True,
                    stop=True,
                )
                y = sb([P, DV], F32, f"y{b}{c}")
                nc.scalar.activation(y[:], bank[:], ACT.Copy, scale=1.0 / 16.0)
                nc.sync.dma_start(out[b, c * P : (c + 1) * P, :], y[:])
